import numpy as np
import ml_dtypes


def mxq(x, axis, fmt="e4m3"):
    dtype, down = {"e4m3": (ml_dtypes.float8_e4m3fn, 7), "e5m2": (ml_dtypes.float8_e5m2, 14)}[fmt]
    v = np.moveaxis(np.asarray(x, np.float32).astype(ml_dtypes.bfloat16).astype(np.float64), axis, -1)
    blocks = v.reshape(v.shape[:-1] + (-1, 32))
    amax = np.abs(blocks).max(-1, keepdims=True)
    byte = np.maximum(np.where(amax > 0, np.frexp(amax)[1] - 1 + 127, 0) - down, 1)
    scale = np.exp2(byte - 127.0)
    codes = (blocks / scale).astype(np.float32).astype(dtype).astype(np.float64)
    return np.moveaxis((codes * scale).reshape(v.shape), -1, axis)


WIDE = False


def mx_kscale(k):
    if not WIDE:
        return np.ones(k)
    levels = np.array([10, -10, 5, -5, 0])
    if k % 512:
        return np.exp2(np.random.permutation(np.resize(levels, k // 32))).repeat(32)
    a = np.empty((k // 512, 16))
    for p in range(k // 512):
        a[p, :8] = np.random.permutation(np.resize(levels, 8))
        for g in range(8):
            far = levels[np.abs(levels - a[p, g]) >= 10]
            a[p, g + 8] = far[np.random.randint(len(far))]
    return np.exp2(a.ravel()).repeat(32)


def f64(x):
    return np.asarray(x).astype(np.float64)


def striped(idx):
    return np.tile(idx.reshape(-1, 16).T, (8, 1)).astype(np.uint16)


def unstriped(offs):
    return offs[:16].T.reshape(-1).astype(np.int64)


def pack_weight(w):
    k, n = w.shape
    w = f64(np.asarray(w, np.float32).astype(ml_dtypes.bfloat16)).reshape(k // 32, 32, n)
    amax = np.abs(w).max(1)
    byte = np.clip(np.where(amax > 0, np.frexp(amax)[1] - 1 + 127 - 7, 1), 1, 254)
    scaled = (w * np.exp2(127.0 - byte)[:, None, :]).reshape(k, n).astype(np.float32)
    words = np.ascontiguousarray(scaled.reshape(k // 512, 128, 4, n).transpose(0, 1, 3, 2)).astype(ml_dtypes.float8_e4m3fn).view(np.uint8)
    return words, np.ascontiguousarray(byte.astype(np.uint8).reshape(k // 512, 16, n))


def unpack_weight(words, scales):
    g, p, n, _ = words.shape
    vals = np.ascontiguousarray(words).view(ml_dtypes.float8_e4m3fn).astype(np.float64) * np.repeat(np.exp2(scales.astype(np.float64) - 127.0), 8, axis=1)[..., None]
    return vals.transpose(0, 1, 3, 2).reshape(g * 512, n)


K, T, S, D, N, H, W, U = 512, 2048, 512, 4, 128, 512, 2048, 1024


def setup_inputs():
    n = np.random.standard_normal
    s = mx_kscale(K)[:, None]
    u = mx_kscale(H)
    packed_xT = pack_weight(n((K, T)) * s)
    packed_eT = pack_weight(n((K, W)) * s)
    return {
        "x_words": packed_xT[0],
        "x_scales": packed_xT[1],
        "w1": (n((K, H)) / np.sqrt(K) / s).astype(np.float32),
        "e_words": packed_eT[0],
        "e_scales": packed_eT[1],
        "w2": (n((K, H)) / np.sqrt(K) / s).astype(np.float32),
        "lo": (np.random.uniform(0.6, 0.9, (H, S))).astype(np.float32),
        "hi": (np.random.uniform(1.1, 1.6, (H, S))).astype(np.float32),
        "wt": (np.random.uniform(0.5, 1.5, (H, U))).astype(np.float32),
        "unit": (np.random.uniform(0.6, 1.4, (H, 1)) * u[:, None]).astype(np.float32),
        "w3": (n((H, N)) / np.sqrt(H) / u[:, None]).astype(np.float32),
        "offs": striped(np.random.permutation(T)[:S]),
        "twin": striped(np.random.permutation(W)[:S]),
        "mini": striped(np.random.permutation(np.concatenate([np.arange(S), np.random.randint(0, S, U - S)]))),
    }


def reference(x_words, x_scales, w1, e_words, e_scales, w2, lo, hi, wt, unit, w3, offs, twin, mini):
    xq = unpack_weight(x_words, x_scales)[:, unstriped(offs)]
    y = mxq(f64(w1), 0, "e4m3").T @ xq
    e_twin = unpack_weight(e_words, e_scales)[:, unstriped(twin)]
    ye = mxq(f64(w2), 0, "e4m3").T @ e_twin
    ratio = np.exp(0.8 * np.tanh(y - ye))
    ym = y.reshape(len(y), -1, D).mean(axis=2)
    adv = y - np.repeat(ym, D, axis=1)
    clip = np.minimum(np.maximum(ratio, f64(lo)), f64(hi))
    sur = np.minimum(ratio * adv, clip * adv)
    om = sur[:, unstriped(mini)]
    hid = f64(unit) * (om * f64(wt))
    return mxq(f64(w3), 0, "e4m3").T @ mxq(hid, 0, "e4m3")

@@ -1,0 +1,237 @@
+from contextlib import ExitStack
+
+import concourse.mybir as mybir
+
+F32 = mybir.dt.float32
+BF16 = mybir.dt.bfloat16
+I32 = mybir.dt.int32
+U32 = mybir.dt.uint32
+U16 = mybir.dt.uint16
+U8 = mybir.dt.uint8
+FP8X4 = mybir.dt.float8_e4m3fn_x4
+ALU = mybir.AluOpType
+ACT = mybir.ActivationFunctionType
+
+P = 128
+PACK = 4
+K, T, S, D, N, H, U = 512, 2048, 512, 4, 128, 512, 1024
+FLOPS = 2 * (2 * K * H * S + H * N * U)
+KIB = 1024
+FUSED_TILES = 2
+CHUNKS = (256, 256, 256, 128, 128)
+
+
+def tile_picked_ydapol_tok_p_kernel(
+    tc, x_words, x_scales, w1, e_words, e_scales, w2, lo, hi, wt, unit, w3, offs, twin, mini, out
+):
+    nc = tc.nc
+    with ExitStack() as ctx:
+        keep = ctx.enter_context(tc.tile_pool(name="keep", bufs=1))
+        work = ctx.enter_context(tc.tile_pool(name="work", bufs=2))
+        loads = ctx.enter_context(tc.tile_pool(name="loads", bufs=1))
+        psum = ctx.enter_context(tc.psum_pool(name="psum", bufs=1))
+
+        def load_words(words, name, offset):
+            table = loads.tile([P, T], I32, name=name, offset=offset)
+            nc.sync.dma_start(table[:], words[0].rearrange("p c r -> p (c r)").bitcast(I32))
+            return table
+
+        def load_scales(scales, name, offset, width, clearer):
+            table = loads.tile([P, width], U8, name=name, offset=offset)
+            clearer.memset(table[:, :T].bitcast(I32), 0)
+            for q in range(4):
+                nc.sync.dma_start(
+                    table[32 * q : 32 * q + 4, :T].bitcast(I32), scales[0, 4 * q : 4 * q + 4, :].bitcast(I32)
+                )
+            return table
+
+        def load_list(src, name):
+            entries = keep.tile([P, src.shape[1]], U16, name=name)
+            nc.sync.dma_start(entries[:], src)
+            return entries
+
+        def load_rows(src, name, offset):
+            rows = loads.tile([P, PACK, src.shape[1]], F32, name=name, offset=offset)
+            nc.sync.dma_start(rows[:], src.rearrange("(p j) c -> p j c", j=PACK))
+            return rows
+
+        def load_dealt(src, t, name, offset):
+            rows = loads.tile([P, src.shape[1]], F32, name=name, offset=offset)
+            nc.sync.dma_start(rows[:], src.rearrange("(p t) c -> t p c", t=PACK)[t])
+            return rows
+
+        offs_sb = load_list(offs, "offs_sb")
+        twin_sb = load_list(twin, "twin_sb")
+        mini_sb = load_list(mini, "mini_sb")
+        x_table = load_words(x_words, "x_table", 64 * KIB)
+
+        def pick_scales(scale_table, entries, name, tag):
+            scales = keep.tile([P, S], U8, name=name, tag=tag, align_bytes=64)
+            nc.vector.tensor_copy(scales[:], scale_table[:, :T].indirect(entries[:]))
+            return scales
+
+        def pick_codes(table, entries, name, tag):
+            codes = keep.tile([P, S], U32, name=name, tag=tag, align_bytes=64)
+            nc.vector.tensor_copy(codes[:], table[:].bitcast(U32).indirect(entries[:]))
+            return codes
+
+        warm_out = keep.tile([P, 1], F32, name="warm_out")
+        warm = loads.tile([P, 18 * KIB // 4], F32, name="warm", offset=0)
+        nc.gpsimd.memset(warm[:, 0:1], 0.0)
+        nc.scalar.activation(warm_out[:], warm[:, 0:1], ACT.Exp)
+        x_scale_table = load_scales(x_scales, "x_scale_table", 18 * KIB, 44 * KIB, nc.vector)
+        x_picked_scales = pick_scales(x_scale_table, offs_sb, "x_picked_scales", "x_picked_scales")
+        w1_raw = load_rows(w1, "w1_raw", 0)
+        w2_raw = load_rows(w2, "w2_raw", 8 * KIB)
+        e_scale_table = load_scales(e_scales, "e_scale_table", 16 * KIB, T, nc.gpsimd)
+        e_table = load_words(e_words, "e_table", 18 * KIB)
+        lo_sb, hi_sb = [], []
+        for t in range(PACK):
+            lo_sb.append(load_dealt(lo, t, "lo%d" % t, (26 + 4 * t) * KIB))
+            hi_sb.append(load_dealt(hi, t, "hi%d" % t, (28 + 4 * t) * KIB))
+        unit_sb = loads.tile([P, PACK], F32, name="unit_sb", offset=60 * KIB)
+        nc.sync.dma_start(unit_sb[:], unit.rearrange("(p t) o -> p (t o)", t=PACK))
+        wt_sb = [load_dealt(wt, t, "wt%d" % t, (42 + 4 * t) * KIB) for t in range(PACK)]
+        w3_raw = load_rows(w3, "w3_raw", 58 * KIB)
+
+        def quantize(grouped, width, name, pool):
+            codes = pool.tile([P, width], U32, name=name + "_codes", align_bytes=64)
+            scales = pool.tile([P, width], U8, name=name + "_scales", align_bytes=64)
+            nc.vector.quantize_mx(out=codes[:].bitcast(FP8X4), scales=scales[:], in_=grouped)
+            return codes, scales
+
+        def quantize_weight_pair(raw, pair, sign, name, on_vector):
+            grouped = keep.tile([P, 2, P, PACK], BF16, name=name + "_grouped", tag="grouped%d" % pair, align_bytes=64)
+            dst = grouped[:].rearrange("p t m j -> p m j t")
+            src = raw[:].rearrange("p j (m t) -> p m j t", t=PACK)[:, :, :, 2 * pair : 2 * pair + 2]
+            if on_vector:
+                nc.vector.tensor_copy(dst, src)
+            else:
+                nc.scalar.activation(dst, src, ACT.Copy, scale=sign)
+            return quantize(grouped[:].rearrange("p t m j -> p (t m j)"), 2 * P, name, keep)
+
+        def product(acc, weight, t, picked, start, stop):
+            codes, scales = weight[t // 2]
+            cols = slice((t % 2) * P, (t % 2 + 1) * P)
+            nc.tensor.matmul_mx(
+                out=acc[:],
+                lhsT=codes[:, cols].bitcast(FP8X4),
+                lhsT_scale=scales[:, cols],
+                rhs=picked[0][:].bitcast(FP8X4),
+                rhs_scale=picked[1][:],
+                start=start,
+                stop=stop,
+            )
+
+        x_picked = (pick_codes(x_table, offs_sb, "x_picked_codes", "x_picked_codes"), x_picked_scales)
+        w1_q = [quantize_weight_pair(w1_raw, pair, 1.0, "w1_%d" % pair, pair == 0) for pair in range(2)]
+
+        adv, y_banks, y_sb = [], [], {}
+
+        def advantage(t):
+            y = psum.tile([P, S], F32, name="y%d" % t)
+            product(y, w1_q, t, x_picked, True, True)
+            y_banks.append(y)
+            grouped_y = y[:].rearrange("p (v d) -> p v d", d=D)
+            if t < 2:
+                total = keep.tile([P, S // D], F32, name="total%d" % t, align_bytes=64)
+            else:
+                total = loads.tile([P, S // D], F32, name="total%d" % t, offset=(18 + t) * KIB)
+            nc.vector.tensor_reduce(total[:], grouped_y, mybir.AxisListType.X, ALU.add)
+            a = keep.tile([P, S], F32, name="adv%d" % t)
+            nc.vector.scalar_tensor_tensor(
+                a[:].rearrange("p (v d) -> p v d", d=D),
+                total[:].unsqueeze(2).to_broadcast([P, S // D, D]),
+                -1.0 / D,
+                grouped_y,
+                ALU.mult,
+                ALU.add,
+            )
+            adv.append(a)
+
+        advantage(0)
+        advantage(1)
+        e_picked_scales = pick_scales(e_scale_table, twin_sb, "e_picked_scales", "total0")
+        w2_q = [quantize_weight_pair(w2_raw, 0, -1.0, "w2_0", False)]
+        e_picked = (pick_codes(e_table, twin_sb, "e_picked_codes", "total1"), e_picked_scales)
+        w2_q.append(quantize_weight_pair(w2_raw, 1, -1.0, "w2_1", False))
+        advantage(2)
+        advantage(3)
+
+        ratio = []
+        for t in range(PACK):
+            acc = psum.tile([P, S], F32, name="diff%d" % (t % 2))
+            if t < FUSED_TILES:
+                product(acc, w1_q, t, x_picked, True, False)
+                product(acc, w2_q, t, e_picked, False, True)
+                diff = acc
+            else:
+                product(acc, w2_q, t, e_picked, True, True)
+                diff = work.tile([P, S], F32, name="diff_sb")
+                nc.vector.tensor_tensor(diff[:], y_sb[t][:], acc[:], ALU.add)
+            bounded = keep.tile([P, S], F32, name="bounded%d" % t, align_bytes=64)
+            nc.scalar.activation(bounded[:], diff[:], ACT.Tanh)
+            r = keep.tile([P, S], F32, name="ratio%d" % t)
+            nc.scalar.activation(r[:], bounded[:], ACT.Exp, scale=0.8)
+            ratio.append(r)
+            if t < PACK - FUSED_TILES:
+                u = t + FUSED_TILES
+                y_sb[u] = keep.tile([P, S], F32, name="y_sb%d" % u, tag="bounded%d" % t, align_bytes=64)
+                nc.scalar.copy(y_sb[u][:], y_banks[u][:])
+
+        sur = []
+        for t in range(PACK):
+            floored = work.tile([P, S], F32, name="floored")
+            nc.vector.tensor_tensor(floored[:], ratio[t][:], lo_sb[t][:], ALU.max)
+            plain = work.tile([P, S], F32, name="plain")
+            nc.vector.tensor_tensor(plain[:], ratio[t][:], adv[t][:], ALU.mult)
+            clip = work.tile([P, S], F32, name="clip")
+            nc.vector.tensor_tensor(clip[:], floored[:], hi_sb[t][:], ALU.min)
+            clipped = work.tile([P, S], F32, name="clipped")
+            nc.vector.tensor_tensor(clipped[:], clip[:], adv[t][:], ALU.mult)
+            s = keep.tile([P, S], F32, name="sur%d" % t)
+            nc.vector.tensor_tensor(s[:], plain[:], clipped[:], ALU.min)
+            sur.append(s)
+
+        weight = keep.tile([P, PACK, U], F32, name="weight", tag="bounded3", align_bytes=64)
+        for t in range(PACK):
+            nc.scalar.activation(weight[:, t, :], wt_sb[t][:], ACT.Copy, scale=unit_sb[:, t : t + 1])
+
+        w3_grouped = keep.tile([P, N, PACK], BF16, name="w3_grouped", tag="bounded2", align_bytes=64)
+        nc.scalar.copy(
+            w3_grouped[:].rearrange("p (c i) j -> p c j i", i=4),
+            w3_raw[:].rearrange("p j (c i) -> p c j i", i=4),
+        )
+        w3_codes, w3_scales = quantize(w3_grouped[:].rearrange("p m j -> p (m j)"), N, "w3", keep)
+
+        r0 = 0
+        for c, n in enumerate(CHUNKS):
+            hid = work.tile([P, PACK, n], F32, name="hid")
+            for t in range(PACK):
+                nc.vector.tensor_tensor(
+                    hid[:, t, :],
+                    sur[t][:].indirect(mini_sb[:, r0 // 16 : (r0 + n) // 16]),
+                    weight[:, t, r0 : r0 + n],
+                    ALU.mult,
+                )
+            grouped = work.tile([P, n, PACK], BF16, name="hid_grouped", align_bytes=64)
+            interleave = nc.vector.tensor_copy if c == len(CHUNKS) - 1 else nc.scalar.copy
+            interleave(
+                grouped[:].rearrange("p (c i) t -> p c t i", i=4),
+                hid[:].rearrange("p t (c i) -> p c t i", i=4),
+            )
+            codes, scales = quantize(grouped[:].rearrange("p r t -> p (r t)"), n, "hid", work)
+            acc = psum.tile([P, n], F32, name="out%d" % (c % 2))
+            nc.tensor.matmul_mx(
+                out=acc[:],
+                lhsT=w3_codes[:].bitcast(FP8X4),
+                lhsT_scale=w3_scales[:],
+                rhs=codes[:].bitcast(FP8X4),
+                rhs_scale=scales[:],
+                start=True,
+                stop=True,
+            )
+            result = work.tile([P, n], F32, name="result")
+            nc.scalar.copy(result[:], acc[:])
+            nc.sync.dma_start(out[:, r0 : r0 + n], result[:])
+            r0 += n

@@ -36,12 +36,12 @@ def tile_picked_ydapol_tok_p_kernel(
             nc.sync.dma_start(table[:], words[0].rearrange("p c r -> p (c r)").bitcast(I32))
             return table
 
-        def load_scales(scales, name, offset, width, clearer):
-            table = loads.tile([P, width], U8, name=name, offset=offset)
-            clearer.memset(table[:, :T].bitcast(I32), 0)
+        def load_scales(scales, name, engine, queue):
+            table = keep.tile([P, T], U8, name=name)
+            engine.memset(table[:].bitcast(I32), 0)
             for q in range(4):
-                nc.sync.dma_start(
-                    table[32 * q : 32 * q + 4, :T].bitcast(I32), scales[0, 4 * q : 4 * q + 4, :].bitcast(I32)
+                queue.dma_start(
+                    table[32 * q : 32 * q + 4, :].bitcast(I32), scales[0, 4 * q : 4 * q + 4, :].bitcast(I32)
                 )
             return table
 
@@ -61,13 +61,13 @@ def tile_picked_ydapol_tok_p_kernel(
             return rows
 
         offs_sb = load_list(offs, "offs_sb")
+        x_table = load_words(x_words, "x_table", 64 * KIB)
         twin_sb = load_list(twin, "twin_sb")
         mini_sb = load_list(mini, "mini_sb")
-        x_table = load_words(x_words, "x_table", 64 * KIB)
 
         def pick_scales(scale_table, entries, name, tag):
             scales = keep.tile([P, S], U8, name=name, tag=tag, align_bytes=64)
-            nc.vector.tensor_copy(scales[:], scale_table[:, :T].indirect(entries[:]))
+            nc.vector.tensor_copy(scales[:], scale_table[:].indirect(entries[:]))
             return scales
 
         def pick_codes(table, entries, name, tag):
@@ -76,14 +76,14 @@ def tile_picked_ydapol_tok_p_kernel(
             return codes
 
         warm_out = keep.tile([P, 1], F32, name="warm_out")
-        warm = loads.tile([P, 18 * KIB // 4], F32, name="warm", offset=0)
+        warm = loads.tile([P, 62 * KIB // 4], F32, name="warm", offset=0)
         nc.gpsimd.memset(warm[:, 0:1], 0.0)
         nc.scalar.activation(warm_out[:], warm[:, 0:1], ACT.Exp)
-        x_scale_table = load_scales(x_scales, "x_scale_table", 18 * KIB, 44 * KIB, nc.vector)
+        x_scale_table = load_scales(x_scales, "x_scale_table", nc.vector, nc.sync)
+        e_scale_table = load_scales(e_scales, "e_scale_table", nc.gpsimd, nc.gpsimd)
         x_picked_scales = pick_scales(x_scale_table, offs_sb, "x_picked_scales", "x_picked_scales")
         w1_raw = load_rows(w1, "w1_raw", 0)
         w2_raw = load_rows(w2, "w2_raw", 8 * KIB)
-        e_scale_table = load_scales(e_scales, "e_scale_table", 16 * KIB, T, nc.gpsimd)
         e_table = load_words(e_words, "e_table", 18 * KIB)
         lo_sb, hi_sb = [], []
         for t in range(PACK):
@@ -100,8 +100,8 @@ def tile_picked_ydapol_tok_p_kernel(
             nc.vector.quantize_mx(out=codes[:].bitcast(FP8X4), scales=scales[:], in_=grouped)
             return codes, scales
 
-        def quantize_weight_pair(raw, pair, sign, name, on_vector):
-            grouped = keep.tile([P, 2, P, PACK], BF16, name=name + "_grouped", tag="grouped%d" % pair, align_bytes=64)
+        def quantize_weight_pair(raw, pair, sign, name, on_vector, tag):
+            grouped = keep.tile([P, 2, P, PACK], BF16, name=name + "_grouped", tag=tag, align_bytes=64)
             dst = grouped[:].rearrange("p t m j -> p m j t")
             src = raw[:].rearrange("p j (m t) -> p m j t", t=PACK)[:, :, :, 2 * pair : 2 * pair + 2]
             if on_vector:
@@ -124,11 +124,14 @@ def tile_picked_ydapol_tok_p_kernel(
             )
 
         x_picked = (pick_codes(x_table, offs_sb, "x_picked_codes", "x_picked_codes"), x_picked_scales)
-        w1_q = [quantize_weight_pair(w1_raw, pair, 1.0, "w1_%d" % pair, pair == 0) for pair in range(2)]
+        w1_q = [quantize_weight_pair(w1_raw, pair, 1.0, "w1_%d" % pair, pair == 0, "grouped%d" % pair) for pair in range(2)]
+        e_picked_scales = pick_scales(e_scale_table, twin_sb, "e_picked_scales", "grouped0")
 
         adv, y_banks, y_sb = [], [], {}
 
-        def advantage(t):
+        totals = []
+
+        def group_sum(t):
             y = psum.tile([P, S], F32, name="y%d" % t)
             product(y, w1_q, t, x_picked, True, True)
             y_banks.append(y)
@@ -138,6 +141,11 @@ def tile_picked_ydapol_tok_p_kernel(
             else:
                 total = loads.tile([P, S // D], F32, name="total%d" % t, offset=(18 + t) * KIB)
             nc.vector.tensor_reduce(total[:], grouped_y, mybir.AxisListType.X, ALU.add)
+            totals.append(total)
+
+        def advantage(t):
+            total = totals[t]
+            grouped_y = y_banks[t][:].rearrange("p (v d) -> p v d", d=D)
             a = keep.tile([P, S], F32, name="adv%d" % t)
             nc.vector.scalar_tensor_tensor(
                 a[:].rearrange("p (v d) -> p v d", d=D),
@@ -149,12 +157,15 @@ def tile_picked_ydapol_tok_p_kernel(
             )
             adv.append(a)
 
+        group_sum(0)
+        group_sum(1)
         advantage(0)
         advantage(1)
-        e_picked_scales = pick_scales(e_scale_table, twin_sb, "e_picked_scales", "total0")
-        w2_q = [quantize_weight_pair(w2_raw, 0, -1.0, "w2_0", False)]
+        w2_q = [quantize_weight_pair(w2_raw, 0, -1.0, "w2_0", False, "grouped1")]
         e_picked = (pick_codes(e_table, twin_sb, "e_picked_codes", "total1"), e_picked_scales)
-        w2_q.append(quantize_weight_pair(w2_raw, 1, -1.0, "w2_1", False))
+        w2_q.append(quantize_weight_pair(w2_raw, 1, -1.0, "w2_1", False, "grouped2"))
+        group_sum(2)
+        group_sum(3)
         advantage(2)
         advantage(3)
 
@@ -179,19 +190,19 @@ def tile_picked_ydapol_tok_p_kernel(
                 y_sb[u] = keep.tile([P, S], F32, name="y_sb%d" % u, tag="bounded%d" % t, align_bytes=64)
                 nc.scalar.copy(y_sb[u][:], y_banks[u][:])
 
-        sur = []
-        for t in range(PACK):
-            floored = work.tile([P, S], F32, name="floored")
-            nc.vector.tensor_tensor(floored[:], ratio[t][:], lo_sb[t][:], ALU.max)
-            plain = work.tile([P, S], F32, name="plain")
-            nc.vector.tensor_tensor(plain[:], ratio[t][:], adv[t][:], ALU.mult)
-            clip = work.tile([P, S], F32, name="clip")
-            nc.vector.tensor_tensor(clip[:], floored[:], hi_sb[t][:], ALU.min)
-            clipped = work.tile([P, S], F32, name="clipped")
-            nc.vector.tensor_tensor(clipped[:], clip[:], adv[t][:], ALU.mult)
-            s = keep.tile([P, S], F32, name="sur%d" % t)
-            nc.vector.tensor_tensor(s[:], plain[:], clipped[:], ALU.min)
-            sur.append(s)
+        floored, plain, clip, clipped, sur = {}, {}, {}, {}, {}
+
+        def step(results, name, t, pool, a, b, op):
+            if 0 <= t < PACK:
+                results[t] = pool.tile([P, S], F32, name=name % t)
+                nc.vector.tensor_tensor(results[t][:], a[t][:], b[t][:], op)
+
+        for t in range(PACK + 1):
+            step(floored, "floored%d", t, keep, ratio, lo_sb, ALU.max)
+            step(clipped, "clipped%d", t - 1, keep, clip, adv, ALU.mult)
+            step(plain, "plain%d", t, keep, ratio, adv, ALU.mult)
+            step(sur, "sur%d", t - 1, keep, plain, clipped, ALU.min)
+            step(clip, "clip%d", t, keep, floored, hi_sb, ALU.min)
 
         weight = keep.tile([P, PACK, U], F32, name="weight", tag="bounded3", align_bytes=64)
         for t in range(PACK):

@@ -36,11 +36,10 @@ def tile_picked_ydapol_tok_p_kernel(
             nc.sync.dma_start(table[:], words[0].rearrange("p c r -> p (c r)").bitcast(I32))
             return table
 
-        def load_scales(scales, name, engine, queue):
-            table = keep.tile([P, T], U8, name=name)
+        def load_scales(scales, table, engine):
             engine.memset(table[:].bitcast(I32), 0)
             for q in range(4):
-                queue.dma_start(
+                nc.sync.dma_start(
                     table[32 * q : 32 * q + 4, :].bitcast(I32), scales[0, 4 * q : 4 * q + 4, :].bitcast(I32)
                 )
             return table
@@ -61,9 +60,9 @@ def tile_picked_ydapol_tok_p_kernel(
             return rows
 
         offs_sb = load_list(offs, "offs_sb")
-        x_table = load_words(x_words, "x_table", 64 * KIB)
         twin_sb = load_list(twin, "twin_sb")
         mini_sb = load_list(mini, "mini_sb")
+        x_table = load_words(x_words, "x_table", 64 * KIB)
 
         def pick_scales(scale_table, entries, name, tag):
             scales = keep.tile([P, S], U8, name=name, tag=tag, align_bytes=64)
@@ -75,15 +74,25 @@ def tile_picked_ydapol_tok_p_kernel(
             nc.vector.tensor_copy(codes[:], table[:].bitcast(U32).indirect(entries[:]))
             return codes
 
-        warm_out = keep.tile([P, 1], F32, name="warm_out")
-        warm = loads.tile([P, 62 * KIB // 4], F32, name="warm", offset=0)
-        nc.gpsimd.memset(warm[:, 0:1], 0.0)
-        nc.scalar.activation(warm_out[:], warm[:, 0:1], ACT.Exp)
-        x_scale_table = load_scales(x_scales, "x_scale_table", nc.vector, nc.sync)
-        e_scale_table = load_scales(e_scales, "e_scale_table", nc.gpsimd, nc.gpsimd)
+        x_scale_table = load_scales(x_scales, keep.tile([P, T], U8, name="x_scale_table"), nc.vector)
         x_picked_scales = pick_scales(x_scale_table, offs_sb, "x_picked_scales", "x_picked_scales")
+        ones = loads.tile([P, 10 * KIB // 4], F32, name="ones", offset=0)
+        diagonal = loads.tile([P, 52 * KIB // 4], F32, name="diagonal", offset=10 * KIB)
+        identity = keep.tile([P, P], F32, name="identity")
+        nc.gpsimd.memset(ones[:, :P], 1.0)
+        nc.gpsimd.affine_select(
+            out=diagonal[:, :P],
+            in_=ones[:, :P],
+            pattern=[[-1, P]],
+            compare_op=ALU.is_equal,
+            fill=0.0,
+            base=0,
+            channel_multiplier=1,
+        )
         w1_raw = load_rows(w1, "w1_raw", 0)
-        w2_raw = load_rows(w2, "w2_raw", 8 * KIB)
+        e_scale_table = load_scales(e_scales, loads.tile([P, T], U8, name="e_scale_table", offset=8 * KIB), nc.gpsimd)
+        nc.scalar.activation(identity[:], diagonal[:, :P], ACT.Copy)
+        w2_raw = load_rows(w2, "w2_raw", 10 * KIB)
         e_table = load_words(e_words, "e_table", 18 * KIB)
         lo_sb, hi_sb = [], []
         for t in range(PACK):
@@ -94,13 +103,16 @@ def tile_picked_ydapol_tok_p_kernel(
         wt_sb = [load_dealt(wt, t, "wt%d" % t, (42 + 4 * t) * KIB) for t in range(PACK)]
         w3_raw = load_rows(w3, "w3_raw", 58 * KIB)
 
-        def quantize(grouped, width, name, pool):
-            codes = pool.tile([P, width], U32, name=name + "_codes", align_bytes=64)
+        def quantize(grouped, width, name, pool, offset=None):
+            if offset is None:
+                codes = pool.tile([P, width], U32, name=name + "_codes", align_bytes=64)
+            else:
+                codes = loads.tile([P, width], U32, name=name + "_codes", align_bytes=64, offset=offset)
             scales = pool.tile([P, width], U8, name=name + "_scales", align_bytes=64)
             nc.vector.quantize_mx(out=codes[:].bitcast(FP8X4), scales=scales[:], in_=grouped)
             return codes, scales
 
-        def quantize_weight_pair(raw, pair, sign, name, on_vector, tag):
+        def quantize_weight_pair(raw, pair, sign, name, on_vector, tag, offset=None):
             grouped = keep.tile([P, 2, P, PACK], BF16, name=name + "_grouped", tag=tag, align_bytes=64)
             dst = grouped[:].rearrange("p t m j -> p m j t")
             src = raw[:].rearrange("p j (m t) -> p m j t", t=PACK)[:, :, :, 2 * pair : 2 * pair + 2]
@@ -108,7 +120,7 @@ def tile_picked_ydapol_tok_p_kernel(
                 nc.vector.tensor_copy(dst, src)
             else:
                 nc.scalar.activation(dst, src, ACT.Copy, scale=sign)
-            return quantize(grouped[:].rearrange("p t m j -> p (t m j)"), 2 * P, name, keep)
+            return quantize(grouped[:].rearrange("p t m j -> p (t m j)"), 2 * P, name, keep, offset)
 
         def product(acc, weight, t, picked, start, stop):
             codes, scales = weight[t // 2]
@@ -135,6 +147,9 @@ def tile_picked_ydapol_tok_p_kernel(
             y = psum.tile([P, S], F32, name="y%d" % t)
             product(y, w1_q, t, x_picked, True, True)
             y_banks.append(y)
+            if t >= FUSED_TILES:
+                y_sb[t] = loads.tile([P, S], F32, name="y_sb%d" % t, offset=(6 + 2 * t) * KIB)
+                nc.scalar.copy(y_sb[t][:], y[:])
             grouped_y = y[:].rearrange("p (v d) -> p v d", d=D)
             if t < 2:
                 total = keep.tile([P, S // D], F32, name="total%d" % t, align_bytes=64)
@@ -146,7 +161,10 @@ def tile_picked_ydapol_tok_p_kernel(
         def advantage(t):
             total = totals[t]
             grouped_y = y_banks[t][:].rearrange("p (v d) -> p v d", d=D)
-            a = keep.tile([P, S], F32, name="adv%d" % t)
+            if t == 1:
+                a = loads.tile([P, S], F32, name="adv%d" % t, offset=18 * KIB)
+            else:
+                a = keep.tile([P, S], F32, name="adv%d" % t)
             nc.vector.scalar_tensor_tensor(
                 a[:].rearrange("p (v d) -> p v d", d=D),
                 total[:].unsqueeze(2).to_broadcast([P, S // D, D]),
@@ -160,35 +178,48 @@ def tile_picked_ydapol_tok_p_kernel(
         group_sum(0)
         group_sum(1)
         advantage(0)
-        advantage(1)
         w2_q = [quantize_weight_pair(w2_raw, 0, -1.0, "w2_0", False, "grouped1")]
-        e_picked = (pick_codes(e_table, twin_sb, "e_picked_codes", "total1"), e_picked_scales)
-        w2_q.append(quantize_weight_pair(w2_raw, 1, -1.0, "w2_1", False, "grouped2"))
+        e_picked = (pick_codes(e_table, twin_sb, "e_picked_codes", "total0"), e_picked_scales)
+        advantage(1)
+        w2_q.append(quantize_weight_pair(w2_raw, 1, -1.0, "w2_1", False, "grouped2", 22 * KIB))
         group_sum(2)
         group_sum(3)
         advantage(2)
         advantage(3)
 
-        ratio = []
-        for t in range(PACK):
-            acc = psum.tile([P, S], F32, name="diff%d" % (t % 2))
-            if t < FUSED_TILES:
-                product(acc, w1_q, t, x_picked, True, False)
-                product(acc, w2_q, t, e_picked, False, True)
-                diff = acc
-            else:
-                product(acc, w2_q, t, e_picked, True, True)
-                diff = work.tile([P, S], F32, name="diff_sb")
-                nc.vector.tensor_tensor(diff[:], y_sb[t][:], acc[:], ALU.add)
+        def transposed_sum(acc, terms):
+            for b in range(S // P):
+                cols = slice(b * P, (b + 1) * P)
+                for n, term in enumerate(terms):
+                    nc.tensor.matmul(
+                        acc[:, cols], term[:, cols], identity[:], start=n == 0, stop=n == len(terms) - 1, is_transpose=True
+                    )
+
+        def exp_tanh(diff, t):
             bounded = keep.tile([P, S], F32, name="bounded%d" % t, align_bytes=64)
             nc.scalar.activation(bounded[:], diff[:], ACT.Tanh)
             r = keep.tile([P, S], F32, name="ratio%d" % t)
             nc.scalar.activation(r[:], bounded[:], ACT.Exp, scale=0.8)
+            return r
+
+        ratio = []
+        for t in range(FUSED_TILES):
+            diff = psum.tile([P, S], F32, name="diff%d" % t)
+            product(diff, w1_q, t, x_picked, True, False)
+            product(diff, w2_q, t, e_picked, False, True)
+            ratio.append(exp_tanh(diff, t))
+        minus_ye = {}
+        for t in range(FUSED_TILES, PACK):
+            acc = psum.tile([P, S], F32, name="minus_ye", tag="out%d" % (t % 2))
+            product(acc, w2_q, t, e_picked, True, True)
+            minus_ye[t] = keep.tile([P, S], F32, name="minus_ye_sb%d" % t)
+            nc.scalar.copy(minus_ye[t][:], acc[:])
+        for t in range(FUSED_TILES, PACK):
+            diff = psum.tile([P, S], F32, name="diff_turned", tag="y%d" % (t % 2))
+            transposed_sum(diff, [y_sb[t], minus_ye[t]])
+            r = psum.tile([P, S], F32, name="ratio_bank", tag="diff%d" % (t % 2))
+            transposed_sum(r, [exp_tanh(diff, t)])
             ratio.append(r)
-            if t < PACK - FUSED_TILES:
-                u = t + FUSED_TILES
-                y_sb[u] = keep.tile([P, S], F32, name="y_sb%d" % u, tag="bounded%d" % t, align_bytes=64)
-                nc.scalar.copy(y_sb[u][:], y_banks[u][:])
 
         floored, plain, clip, clipped, sur = {}, {}, {}, {}, {}
 
@@ -243,6 +274,6 @@ def tile_picked_ydapol_tok_p_kernel(
                 stop=True,
             )
             result = work.tile([P, n], F32, name="result")
-            nc.scalar.copy(result[:], acc[:])
+            interleave(result[:], acc[:])
             nc.sync.dma_start(out[:, r0 : r0 + n], result[:])
             r0 += n

@@ -69,9 +69,13 @@ def tile_picked_ydapol_tok_p_kernel(
             nc.vector.tensor_copy(scales[:], scale_table[:].indirect(entries[:]))
             return scales
 
-        def pick_codes(table, entries, name, tag):
+        def pick_codes(table, entries, name, tag, parts):
             codes = keep.tile([P, S], U32, name=name, tag=tag, align_bytes=64)
-            nc.vector.tensor_copy(codes[:], table[:].bitcast(U32).indirect(entries[:]))
+            n = S // parts
+            for j0 in range(0, S, n):
+                nc.vector.tensor_copy(
+                    codes[:, j0 : j0 + n], table[:].bitcast(U32).indirect(entries[:, j0 // 16 : (j0 + n) // 16])
+                )
             return codes
 
         x_scale_table = load_scales(x_scales, keep.tile([P, T], U8, name="x_scale_table"), nc.vector)
@@ -122,20 +126,20 @@ def tile_picked_ydapol_tok_p_kernel(
                 nc.scalar.activation(dst, src, ACT.Copy, scale=sign)
             return quantize(grouped[:].rearrange("p t m j -> p (t m j)"), 2 * P, name, keep, offset)
 
-        def product(acc, weight, t, picked, start, stop):
+        def product(acc, weight, t, picked, start, stop, tokens=slice(0, S)):
             codes, scales = weight[t // 2]
             cols = slice((t % 2) * P, (t % 2 + 1) * P)
             nc.tensor.matmul_mx(
                 out=acc[:],
                 lhsT=codes[:, cols].bitcast(FP8X4),
                 lhsT_scale=scales[:, cols],
-                rhs=picked[0][:].bitcast(FP8X4),
-                rhs_scale=picked[1][:],
+                rhs=picked[0][:, tokens].bitcast(FP8X4),
+                rhs_scale=picked[1][:, tokens],
                 start=start,
                 stop=stop,
             )
 
-        x_picked = (pick_codes(x_table, offs_sb, "x_picked_codes", "x_picked_codes"), x_picked_scales)
+        x_picked = (pick_codes(x_table, offs_sb, "x_picked_codes", "x_picked_codes", 1), x_picked_scales)
         w1_q = [quantize_weight_pair(w1_raw, pair, 1.0, "w1_%d" % pair, pair == 0, "grouped%d" % pair) for pair in range(2)]
         e_picked_scales = pick_scales(e_scale_table, twin_sb, "e_picked_scales", "grouped0")
 
@@ -151,20 +155,23 @@ def tile_picked_ydapol_tok_p_kernel(
                 y_sb[t] = loads.tile([P, S], F32, name="y_sb%d" % t, offset=(6 + 2 * t) * KIB)
                 nc.scalar.copy(y_sb[t][:], y[:])
             grouped_y = y[:].rearrange("p (v d) -> p v d", d=D)
-            if t < 2:
-                total = keep.tile([P, S // D], F32, name="total%d" % t, align_bytes=64)
+            total = keep.tile([P, S // D], F32, name="total%d" % t, align_bytes=64)
+            if t < FUSED_TILES:
+                nc.vector.tensor_reduce(total[:], grouped_y, mybir.AxisListType.X, ALU.add)
             else:
-                total = loads.tile([P, S // D], F32, name="total%d" % t, offset=(18 + t) * KIB)
-            nc.vector.tensor_reduce(total[:], grouped_y, mybir.AxisListType.X, ALU.add)
+                members = y_sb[t][:].rearrange("p (v d) -> p v d", d=D)
+                pairs = work.tile([P, S // D, 2], F32, name="pairs")
+                nc.gpsimd.tensor_tensor(pairs[:], members[:, :, 0:2], members[:, :, 2:4], ALU.add)
+                nc.gpsimd.tensor_tensor(total[:], pairs[:, :, 0], pairs[:, :, 1], ALU.add)
             totals.append(total)
 
         def advantage(t):
             total = totals[t]
             grouped_y = y_banks[t][:].rearrange("p (v d) -> p v d", d=D)
-            if t == 1:
-                a = loads.tile([P, S], F32, name="adv%d" % t, offset=18 * KIB)
-            else:
+            if t == 0:
                 a = keep.tile([P, S], F32, name="adv%d" % t)
+            else:
+                a = loads.tile([P, S], F32, name="adv%d" % t, offset=(16 + 2 * t) * KIB)
             nc.vector.scalar_tensor_tensor(
                 a[:].rearrange("p (v d) -> p v d", d=D),
                 total[:].unsqueeze(2).to_broadcast([P, S // D, D]),
@@ -179,9 +186,9 @@ def tile_picked_ydapol_tok_p_kernel(
         group_sum(1)
         advantage(0)
         w2_q = [quantize_weight_pair(w2_raw, 0, -1.0, "w2_0", False, "grouped1")]
-        e_picked = (pick_codes(e_table, twin_sb, "e_picked_codes", "total0"), e_picked_scales)
+        e_picked = (pick_codes(e_table, twin_sb, "e_picked_codes", "total0", 2), e_picked_scales)
         advantage(1)
-        w2_q.append(quantize_weight_pair(w2_raw, 1, -1.0, "w2_1", False, "grouped2", 22 * KIB))
+        w2_q.append(quantize_weight_pair(w2_raw, 1, -1.0, "w2_1", False, "grouped2", 24 * KIB))
         group_sum(2)
         group_sum(3)
         advantage(2)
@@ -195,19 +202,25 @@ def tile_picked_ydapol_tok_p_kernel(
                         acc[:, cols], term[:, cols], identity[:], start=n == 0, stop=n == len(terms) - 1, is_transpose=True
                     )
 
-        def exp_tanh(diff, t):
+        def exp_tanh(parts, t):
             bounded = keep.tile([P, S], F32, name="bounded%d" % t, align_bytes=64)
-            nc.scalar.activation(bounded[:], diff[:], ACT.Tanh)
             r = keep.tile([P, S], F32, name="ratio%d" % t)
-            nc.scalar.activation(r[:], bounded[:], ACT.Exp, scale=0.8)
+            for diff, tokens in parts:
+                nc.scalar.activation(bounded[:, tokens], diff[:], ACT.Tanh)
+                nc.scalar.activation(r[:, tokens], bounded[:, tokens], ACT.Exp, scale=0.8)
             return r
 
         ratio = []
-        for t in range(FUSED_TILES):
-            diff = psum.tile([P, S], F32, name="diff%d" % t)
-            product(diff, w1_q, t, x_picked, True, False)
-            product(diff, w2_q, t, e_picked, False, True)
-            ratio.append(exp_tanh(diff, t))
+        for t, banks in enumerate((("diff0", "y0"), ("diff1",))):
+            parts = []
+            n = S // len(banks)
+            for h, bank in enumerate(banks):
+                tokens = slice(h * n, (h + 1) * n)
+                diff = psum.tile([P, n], F32, name="diff", tag=bank)
+                product(diff, w1_q, t, x_picked, True, False, tokens)
+                product(diff, w2_q, t, e_picked, False, True, tokens)
+                parts.append((diff, tokens))
+            ratio.append(exp_tanh(parts, t))
         minus_ye = {}
         for t in range(FUSED_TILES, PACK):
             acc = psum.tile([P, S], F32, name="minus_ye", tag="out%d" % (t % 2))
@@ -218,7 +231,7 @@ def tile_picked_ydapol_tok_p_kernel(
             diff = psum.tile([P, S], F32, name="diff_turned", tag="y%d" % (t % 2))
             transposed_sum(diff, [y_sb[t], minus_ye[t]])
             r = psum.tile([P, S], F32, name="ratio_bank", tag="diff%d" % (t % 2))
-            transposed_sum(r, [exp_tanh(diff, t)])
+            transposed_sum(r, [exp_tanh([(diff, slice(0, S))], t)])
             ratio.append(r)
 
         floored, plain, clip, clipped, sur = {}, {}, {}, {}, {}

@@ -14,11 +14,22 @@ ACT = mybir.ActivationFunctionType
 
 P = 128
 PACK = 4
+QUADRANTS = 4
+STRIPE = 16
+LINE = 4
 K, T, S, D, N, H, U = 512, 2048, 512, 4, 128, 512, 1024
 FLOPS = 2 * (2 * K * H * S + H * N * U)
-KIB = 1024
+
 FUSED_TILES = 2
 CHUNKS = (256, 256, 256, 128, 128)
+
+KIB = 1024
+W1_AT, W2_AT, E_SCALES_AT = 0, 8 * KIB, 16 * KIB
+E_WORDS_AT, BOUNDS_AT, WT_AT, W3_AT, UNIT_AT = 18 * KIB, 26 * KIB, 42 * KIB, 58 * KIB, 60 * KIB
+X_WORDS_AT = 64 * KIB
+FIRST_HELD = (W1_AT, E_WORDS_AT)
+SECOND_HELD = (E_WORDS_AT, 62 * KIB)
+ROW_BYTES = 4 * S
 
 
 def tile_picked_ydapol_tok_p_kernel(
@@ -38,7 +49,7 @@ def tile_picked_ydapol_tok_p_kernel(
 
         def load_scales(scales, table, engine):
             engine.memset(table[:].bitcast(I32), 0)
-            for q in range(4):
+            for q in range(QUADRANTS):
                 nc.sync.dma_start(
                     table[32 * q : 32 * q + 4, :].bitcast(I32), scales[0, 4 * q : 4 * q + 4, :].bitcast(I32)
                 )
@@ -49,20 +60,18 @@ def tile_picked_ydapol_tok_p_kernel(
             nc.sync.dma_start(entries[:], src)
             return entries
 
-        def load_rows(src, name, offset):
+        def load_weight(src, name, offset):
             rows = loads.tile([P, PACK, src.shape[1]], F32, name=name, offset=offset)
             nc.sync.dma_start(rows[:], src.rearrange("(p j) c -> p j c", j=PACK))
             return rows
 
-        def load_dealt(src, t, name, offset):
+        def load_hidden_tile(src, t, name, offset):
             rows = loads.tile([P, src.shape[1]], F32, name=name, offset=offset)
             nc.sync.dma_start(rows[:], src.rearrange("(p t) c -> t p c", t=PACK)[t])
             return rows
 
-        offs_sb = load_list(offs, "offs_sb")
-        twin_sb = load_list(twin, "twin_sb")
-        mini_sb = load_list(mini, "mini_sb")
-        x_table = load_words(x_words, "x_table", 64 * KIB)
+        def covering(span, name):
+            return loads.tile([P, (span[1] - span[0]) // 4], F32, name=name, offset=span[0])
 
         def pick_scales(scale_table, entries, name, tag):
             scales = keep.tile([P, S], U8, name=name, tag=tag, align_bytes=64)
@@ -71,17 +80,55 @@ def tile_picked_ydapol_tok_p_kernel(
 
         def pick_codes(table, entries, name, tag, parts):
             codes = keep.tile([P, S], U32, name=name, tag=tag, align_bytes=64)
-            n = S // parts
-            for j0 in range(0, S, n):
+            width = S // parts
+            for j0 in range(0, S, width):
                 nc.vector.tensor_copy(
-                    codes[:, j0 : j0 + n], table[:].bitcast(U32).indirect(entries[:, j0 // 16 : (j0 + n) // 16])
+                    codes[:, j0 : j0 + width],
+                    table[:].bitcast(U32).indirect(entries[:, j0 // STRIPE : (j0 + width) // STRIPE]),
                 )
             return codes
 
+        def quantize(grouped, codes, name, pool):
+            scales = pool.tile([P, codes.shape[1]], U8, name=name + "_scales", align_bytes=64)
+            nc.vector.quantize_mx(out=codes[:].bitcast(FP8X4), scales=scales[:], in_=grouped)
+            return codes, scales
+
+        def negated_copy(dst, src):
+            nc.scalar.activation(dst, src, ACT.Copy, scale=-1.0)
+
+        def plain_copy(dst, src):
+            nc.scalar.activation(dst, src, ACT.Copy, scale=1.0)
+
+        def quantize_weight_pair(raw, pair, name, interleave, tag, codes_pool, codes_offset):
+            grouped = keep.tile([P, 2, P, PACK], BF16, name=name + "_grouped", tag=tag, align_bytes=64)
+            interleave(
+                grouped[:].rearrange("p t m j -> p m j t"),
+                raw[:].rearrange("p j (m t) -> p m j t", t=PACK)[:, :, :, 2 * pair : 2 * pair + 2],
+            )
+            codes = codes_pool.tile([P, 2 * P], U32, name=name + "_codes", align_bytes=64, offset=codes_offset)
+            return quantize(grouped[:].rearrange("p t m j -> p (t m j)"), codes, name, keep)
+
+        def product(acc, weight_pairs, t, picked, start, stop, tokens=slice(0, S)):
+            codes, scales = weight_pairs[t // 2]
+            channels = slice((t % 2) * P, (t % 2 + 1) * P)
+            nc.tensor.matmul_mx(
+                out=acc[:],
+                lhsT=codes[:, channels].bitcast(FP8X4),
+                lhsT_scale=scales[:, channels],
+                rhs=picked[0][:, tokens].bitcast(FP8X4),
+                rhs_scale=picked[1][:, tokens],
+                start=start,
+                stop=stop,
+            )
+
+        offs_sb = load_list(offs, "offs_sb")
+        twin_sb = load_list(twin, "twin_sb")
+        mini_sb = load_list(mini, "mini_sb")
+        x_table = load_words(x_words, "x_table", X_WORDS_AT)
         x_scale_table = load_scales(x_scales, keep.tile([P, T], U8, name="x_scale_table"), nc.vector)
         x_picked_scales = pick_scales(x_scale_table, offs_sb, "x_picked_scales", "x_picked_scales")
-        ones = loads.tile([P, 10 * KIB // 4], F32, name="ones", offset=0)
-        diagonal = loads.tile([P, 52 * KIB // 4], F32, name="diagonal", offset=10 * KIB)
+        ones = covering(FIRST_HELD, "ones")
+        diagonal = covering(SECOND_HELD, "diagonal")
         identity = keep.tile([P, P], F32, name="identity")
         nc.gpsimd.memset(ones[:, :P], 1.0)
         nc.gpsimd.affine_select(
@@ -93,160 +140,134 @@ def tile_picked_ydapol_tok_p_kernel(
             base=0,
             channel_multiplier=1,
         )
-        w1_raw = load_rows(w1, "w1_raw", 0)
-        e_scale_table = load_scales(e_scales, loads.tile([P, T], U8, name="e_scale_table", offset=8 * KIB), nc.gpsimd)
+        w1_raw = load_weight(w1, "w1_raw", W1_AT)
+        w2_raw = load_weight(w2, "w2_raw", W2_AT)
+        e_scale_table = load_scales(
+            e_scales, loads.tile([P, T], U8, name="e_scale_table", offset=E_SCALES_AT), nc.gpsimd
+        )
         nc.scalar.activation(identity[:], diagonal[:, :P], ACT.Copy)
-        w2_raw = load_rows(w2, "w2_raw", 10 * KIB)
-        e_table = load_words(e_words, "e_table", 18 * KIB)
+        e_table = load_words(e_words, "e_table", E_WORDS_AT)
         lo_sb, hi_sb = [], []
         for t in range(PACK):
-            lo_sb.append(load_dealt(lo, t, "lo%d" % t, (26 + 4 * t) * KIB))
-            hi_sb.append(load_dealt(hi, t, "hi%d" % t, (28 + 4 * t) * KIB))
-        unit_sb = loads.tile([P, PACK], F32, name="unit_sb", offset=60 * KIB)
+            lo_sb.append(load_hidden_tile(lo, t, "lo%d" % t, BOUNDS_AT + 2 * t * ROW_BYTES))
+            hi_sb.append(load_hidden_tile(hi, t, "hi%d" % t, BOUNDS_AT + (2 * t + 1) * ROW_BYTES))
+        unit_sb = loads.tile([P, PACK], F32, name="unit_sb", offset=UNIT_AT)
         nc.sync.dma_start(unit_sb[:], unit.rearrange("(p t) o -> p (t o)", t=PACK))
-        wt_sb = [load_dealt(wt, t, "wt%d" % t, (42 + 4 * t) * KIB) for t in range(PACK)]
-        w3_raw = load_rows(w3, "w3_raw", 58 * KIB)
-
-        def quantize(grouped, width, name, pool, offset=None):
-            if offset is None:
-                codes = pool.tile([P, width], U32, name=name + "_codes", align_bytes=64)
-            else:
-                codes = loads.tile([P, width], U32, name=name + "_codes", align_bytes=64, offset=offset)
-            scales = pool.tile([P, width], U8, name=name + "_scales", align_bytes=64)
-            nc.vector.quantize_mx(out=codes[:].bitcast(FP8X4), scales=scales[:], in_=grouped)
-            return codes, scales
-
-        def quantize_weight_pair(raw, pair, sign, name, on_vector, tag, offset=None):
-            grouped = keep.tile([P, 2, P, PACK], BF16, name=name + "_grouped", tag=tag, align_bytes=64)
-            dst = grouped[:].rearrange("p t m j -> p m j t")
-            src = raw[:].rearrange("p j (m t) -> p m j t", t=PACK)[:, :, :, 2 * pair : 2 * pair + 2]
-            if on_vector:
-                nc.vector.tensor_copy(dst, src)
-            else:
-                nc.scalar.activation(dst, src, ACT.Copy, scale=sign)
-            return quantize(grouped[:].rearrange("p t m j -> p (t m j)"), 2 * P, name, keep, offset)
-
-        def product(acc, weight, t, picked, start, stop, tokens=slice(0, S)):
-            codes, scales = weight[t // 2]
-            cols = slice((t % 2) * P, (t % 2 + 1) * P)
-            nc.tensor.matmul_mx(
-                out=acc[:],
-                lhsT=codes[:, cols].bitcast(FP8X4),
-                lhsT_scale=scales[:, cols],
-                rhs=picked[0][:, tokens].bitcast(FP8X4),
-                rhs_scale=picked[1][:, tokens],
-                start=start,
-                stop=stop,
-            )
+        wt_sb = [load_hidden_tile(wt, t, "wt%d" % t, WT_AT + t * 4 * U) for t in range(PACK)]
+        w3_raw = load_weight(w3, "w3_raw", W3_AT)
 
         x_picked = (pick_codes(x_table, offs_sb, "x_picked_codes", "x_picked_codes", 1), x_picked_scales)
-        w1_q = [quantize_weight_pair(w1_raw, pair, 1.0, "w1_%d" % pair, pair == 0, "grouped%d" % pair) for pair in range(2)]
-        e_picked_scales = pick_scales(e_scale_table, twin_sb, "e_picked_scales", "grouped0")
+        w1_pairs = [
+            quantize_weight_pair(w1_raw, 0, "w1_0", nc.vector.tensor_copy, "grouped0", keep, None),
+            quantize_weight_pair(w1_raw, 1, "w1_1", plain_copy, "grouped1", keep, None),
+        ]
 
-        adv, y_banks, y_sb = [], [], {}
-
-        totals = []
+        y_banks, y_sb, totals, adv = [], {}, [], []
 
         def group_sum(t):
             y = psum.tile([P, S], F32, name="y%d" % t)
-            product(y, w1_q, t, x_picked, True, True)
+            product(y, w1_pairs, t, x_picked, True, True)
             y_banks.append(y)
-            if t >= FUSED_TILES:
-                y_sb[t] = loads.tile([P, S], F32, name="y_sb%d" % t, offset=(6 + 2 * t) * KIB)
-                nc.scalar.copy(y_sb[t][:], y[:])
-            grouped_y = y[:].rearrange("p (v d) -> p v d", d=D)
-            total = keep.tile([P, S // D], F32, name="total%d" % t, align_bytes=64)
             if t < FUSED_TILES:
-                nc.vector.tensor_reduce(total[:], grouped_y, mybir.AxisListType.X, ALU.add)
+                total = keep.tile([P, S // D], F32, name="total%d" % t, align_bytes=64)
+                nc.vector.tensor_reduce(
+                    total[:], y[:].rearrange("p (v d) -> p v d", d=D), mybir.AxisListType.X, ALU.add
+                )
             else:
+                y_sb[t] = loads.tile([P, S], F32, name="y_sb%d" % t, offset=W2_AT + (t - FUSED_TILES) * ROW_BYTES)
+                nc.scalar.copy(y_sb[t][:], y[:])
+                total = keep.tile([P, S // D], F32, name="total%d" % t, align_bytes=64)
                 members = y_sb[t][:].rearrange("p (v d) -> p v d", d=D)
-                pairs = work.tile([P, S // D, 2], F32, name="pairs")
-                nc.gpsimd.tensor_tensor(pairs[:], members[:, :, 0:2], members[:, :, 2:4], ALU.add)
-                nc.gpsimd.tensor_tensor(total[:], pairs[:, :, 0], pairs[:, :, 1], ALU.add)
+                half_sums = work.tile([P, S // D, 2], F32, name="pairs")
+                nc.gpsimd.tensor_tensor(half_sums[:], members[:, :, 0:2], members[:, :, 2:4], ALU.add)
+                nc.gpsimd.tensor_tensor(total[:], half_sums[:, :, 0], half_sums[:, :, 1], ALU.add)
             totals.append(total)
 
-        def advantage(t):
-            total = totals[t]
-            grouped_y = y_banks[t][:].rearrange("p (v d) -> p v d", d=D)
-            if t == 0:
-                a = keep.tile([P, S], F32, name="adv%d" % t)
-            else:
-                a = loads.tile([P, S], F32, name="adv%d" % t, offset=(16 + 2 * t) * KIB)
+        def advantage(t, pool, offset):
+            values = pool.tile([P, S], F32, name="adv%d" % t, offset=offset)
             nc.vector.scalar_tensor_tensor(
-                a[:].rearrange("p (v d) -> p v d", d=D),
-                total[:].unsqueeze(2).to_broadcast([P, S // D, D]),
+                values[:].rearrange("p (v d) -> p v d", d=D),
+                totals[t][:].unsqueeze(2).to_broadcast([P, S // D, D]),
                 -1.0 / D,
-                grouped_y,
+                y_banks[t][:].rearrange("p (v d) -> p v d", d=D),
                 ALU.mult,
                 ALU.add,
             )
-            adv.append(a)
+            adv.append(values)
 
         group_sum(0)
         group_sum(1)
-        advantage(0)
-        w2_q = [quantize_weight_pair(w2_raw, 0, -1.0, "w2_0", False, "grouped1")]
-        e_picked = (pick_codes(e_table, twin_sb, "e_picked_codes", "total0", 2), e_picked_scales)
-        advantage(1)
-        w2_q.append(quantize_weight_pair(w2_raw, 1, -1.0, "w2_1", False, "grouped2", 24 * KIB))
+        advantage(0, keep, None)
+        e_picked_scales = pick_scales(e_scale_table, twin_sb, "e_picked_scales", "total0")
+        minus_w2_pairs = [quantize_weight_pair(w2_raw, 0, "w2_0", negated_copy, "grouped1", keep, None)]
+        e_picked = (pick_codes(e_table, twin_sb, "e_picked_codes", "grouped1", 2), e_picked_scales)
+        advantage(1, loads, E_WORDS_AT)
+        minus_w2_pairs.append(
+            quantize_weight_pair(w2_raw, 1, "w2_1", negated_copy, "grouped2", loads, E_WORDS_AT + 3 * ROW_BYTES)
+        )
         group_sum(2)
         group_sum(3)
-        advantage(2)
-        advantage(3)
+        advantage(2, loads, E_WORDS_AT + ROW_BYTES)
+        advantage(3, loads, E_WORDS_AT + 2 * ROW_BYTES)
 
         def transposed_sum(acc, terms):
             for b in range(S // P):
-                cols = slice(b * P, (b + 1) * P)
-                for n, term in enumerate(terms):
+                block = slice(b * P, (b + 1) * P)
+                for index, term in enumerate(terms):
                     nc.tensor.matmul(
-                        acc[:, cols], term[:, cols], identity[:], start=n == 0, stop=n == len(terms) - 1, is_transpose=True
+                        acc[:, block],
+                        term[:, block],
+                        identity[:],
+                        start=index == 0,
+                        stop=index == len(terms) - 1,
+                        is_transpose=True,
                     )
 
         def exp_tanh(parts, t):
             bounded = keep.tile([P, S], F32, name="bounded%d" % t, align_bytes=64)
-            r = keep.tile([P, S], F32, name="ratio%d" % t)
+            values = keep.tile([P, S], F32, name="ratio%d" % t)
             for diff, tokens in parts:
                 nc.scalar.activation(bounded[:, tokens], diff[:], ACT.Tanh)
-                nc.scalar.activation(r[:, tokens], bounded[:, tokens], ACT.Exp, scale=0.8)
-            return r
+                nc.scalar.activation(values[:, tokens], bounded[:, tokens], ACT.Exp, scale=0.8)
+            return values
 
         ratio = []
         for t, banks in enumerate((("diff0", "y0"), ("diff1",))):
             parts = []
-            n = S // len(banks)
-            for h, bank in enumerate(banks):
-                tokens = slice(h * n, (h + 1) * n)
-                diff = psum.tile([P, n], F32, name="diff", tag=bank)
-                product(diff, w1_q, t, x_picked, True, False, tokens)
-                product(diff, w2_q, t, e_picked, False, True, tokens)
+            width = S // len(banks)
+            for half, bank in enumerate(banks):
+                tokens = slice(half * width, (half + 1) * width)
+                diff = psum.tile([P, width], F32, name="diff", tag=bank)
+                product(diff, w1_pairs, t, x_picked, True, False, tokens)
+                product(diff, minus_w2_pairs, t, e_picked, False, True, tokens)
                 parts.append((diff, tokens))
             ratio.append(exp_tanh(parts, t))
         minus_ye = {}
         for t in range(FUSED_TILES, PACK):
-            acc = psum.tile([P, S], F32, name="minus_ye", tag="out%d" % (t % 2))
-            product(acc, w2_q, t, e_picked, True, True)
+            minus_ye_bank = psum.tile([P, S], F32, name="minus_ye", tag="out%d" % (t % 2))
+            product(minus_ye_bank, minus_w2_pairs, t, e_picked, True, True)
             minus_ye[t] = keep.tile([P, S], F32, name="minus_ye_sb%d" % t)
-            nc.scalar.copy(minus_ye[t][:], acc[:])
+            nc.scalar.copy(minus_ye[t][:], minus_ye_bank[:])
         for t in range(FUSED_TILES, PACK):
-            diff = psum.tile([P, S], F32, name="diff_turned", tag="y%d" % (t % 2))
-            transposed_sum(diff, [y_sb[t], minus_ye[t]])
-            r = psum.tile([P, S], F32, name="ratio_bank", tag="diff%d" % (t % 2))
-            transposed_sum(r, [exp_tanh([(diff, slice(0, S))], t)])
-            ratio.append(r)
+            diff_turned = psum.tile([P, S], F32, name="diff_turned", tag="y%d" % (t % 2))
+            transposed_sum(diff_turned, [y_sb[t], minus_ye[t]])
+            ratio_bank = psum.tile([P, S], F32, name="ratio_bank", tag="diff%d" % (t % 2))
+            transposed_sum(ratio_bank, [exp_tanh([(diff_turned, slice(0, S))], t)])
+            ratio.append(ratio_bank)
 
         floored, plain, clip, clipped, sur = {}, {}, {}, {}, {}
 
-        def step(results, name, t, pool, a, b, op):
+        def step(results, name, t, first, second, op):
             if 0 <= t < PACK:
-                results[t] = pool.tile([P, S], F32, name=name % t)
-                nc.vector.tensor_tensor(results[t][:], a[t][:], b[t][:], op)
+                results[t] = keep.tile([P, S], F32, name=name % t)
+                nc.vector.tensor_tensor(results[t][:], first[t][:], second[t][:], op)
 
         for t in range(PACK + 1):
-            step(floored, "floored%d", t, keep, ratio, lo_sb, ALU.max)
-            step(clipped, "clipped%d", t - 1, keep, clip, adv, ALU.mult)
-            step(plain, "plain%d", t, keep, ratio, adv, ALU.mult)
-            step(sur, "sur%d", t - 1, keep, plain, clipped, ALU.min)
-            step(clip, "clip%d", t, keep, floored, hi_sb, ALU.min)
+            step(floored, "floored%d", t, ratio, lo_sb, ALU.max)
+            step(clipped, "clipped%d", t - 1, clip, adv, ALU.mult)
+            step(plain, "plain%d", t, ratio, adv, ALU.mult)
+            step(sur, "sur%d", t - 1, plain, clipped, ALU.min)
+            step(clip, "clip%d", t, floored, hi_sb, ALU.min)
 
         weight = keep.tile([P, PACK, U], F32, name="weight", tag="bounded3", align_bytes=64)
         for t in range(PACK):
@@ -254,39 +275,41 @@ def tile_picked_ydapol_tok_p_kernel(
 
         w3_grouped = keep.tile([P, N, PACK], BF16, name="w3_grouped", tag="bounded2", align_bytes=64)
         nc.scalar.copy(
-            w3_grouped[:].rearrange("p (c i) j -> p c j i", i=4),
-            w3_raw[:].rearrange("p j (c i) -> p c j i", i=4),
+            w3_grouped[:].rearrange("p (c i) j -> p c j i", i=LINE),
+            w3_raw[:].rearrange("p j (c i) -> p c j i", i=LINE),
         )
-        w3_codes, w3_scales = quantize(w3_grouped[:].rearrange("p m j -> p (m j)"), N, "w3", keep)
+        w3_codes = keep.tile([P, N], U32, name="w3_codes", align_bytes=64)
+        w3_codes, w3_scales = quantize(w3_grouped[:].rearrange("p m j -> p (m j)"), w3_codes, "w3", keep)
 
         r0 = 0
-        for c, n in enumerate(CHUNKS):
-            hid = work.tile([P, PACK, n], F32, name="hid")
+        for c, width in enumerate(CHUNKS):
+            copy = nc.vector.tensor_copy if c == len(CHUNKS) - 1 else nc.scalar.copy
+            hid = work.tile([P, PACK, width], F32, name="hid")
             for t in range(PACK):
                 nc.vector.tensor_tensor(
                     hid[:, t, :],
-                    sur[t][:].indirect(mini_sb[:, r0 // 16 : (r0 + n) // 16]),
-                    weight[:, t, r0 : r0 + n],
+                    sur[t][:].indirect(mini_sb[:, r0 // STRIPE : (r0 + width) // STRIPE]),
+                    weight[:, t, r0 : r0 + width],
                     ALU.mult,
                 )
-            grouped = work.tile([P, n, PACK], BF16, name="hid_grouped", align_bytes=64)
-            interleave = nc.vector.tensor_copy if c == len(CHUNKS) - 1 else nc.scalar.copy
-            interleave(
-                grouped[:].rearrange("p (c i) t -> p c t i", i=4),
-                hid[:].rearrange("p t (c i) -> p c t i", i=4),
+            hid_grouped = work.tile([P, width, PACK], BF16, name="hid_grouped", align_bytes=64)
+            copy(
+                hid_grouped[:].rearrange("p (c i) t -> p c t i", i=LINE),
+                hid[:].rearrange("p t (c i) -> p c t i", i=LINE),
             )
-            codes, scales = quantize(grouped[:].rearrange("p r t -> p (r t)"), n, "hid", work)
-            acc = psum.tile([P, n], F32, name="out%d" % (c % 2))
+            hid_codes = work.tile([P, width], U32, name="hid_codes", align_bytes=64)
+            hid_codes, hid_scales = quantize(hid_grouped[:].rearrange("p r t -> p (r t)"), hid_codes, "hid", work)
+            out_bank = psum.tile([P, width], F32, name="out%d" % (c % 2))
             nc.tensor.matmul_mx(
-                out=acc[:],
+                out=out_bank[:],
                 lhsT=w3_codes[:].bitcast(FP8X4),
                 lhsT_scale=w3_scales[:],
-                rhs=codes[:].bitcast(FP8X4),
-                rhs_scale=scales[:],
+                rhs=hid_codes[:].bitcast(FP8X4),
+                rhs_scale=hid_scales[:],
                 start=True,
                 stop=True,
             )
-            result = work.tile([P, n], F32, name="result")
-            interleave(result[:], acc[:])
-            nc.sync.dma_start(out[:, r0 : r0 + n], result[:])
-            r0 += n
+            result = work.tile([P, width], F32, name="result")
+            copy(result[:], out_bank[:])
+            nc.sync.dma_start(out[:, r0 : r0 + width], result[:])
+            r0 += width

from contextlib import ExitStack

import concourse.mybir as mybir

F32 = mybir.dt.float32
BF16 = mybir.dt.bfloat16
I32 = mybir.dt.int32
U32 = mybir.dt.uint32
U16 = mybir.dt.uint16
U8 = mybir.dt.uint8
FP8X4 = mybir.dt.float8_e4m3fn_x4
ALU = mybir.AluOpType
ACT = mybir.ActivationFunctionType

P = 128
PACK = 4
QUADRANTS = 4
STRIPE = 16
LINE = 4
K, T, S, D, N, H, U = 512, 2048, 512, 4, 128, 512, 1024
FLOPS = 2 * (2 * K * H * S + H * N * U)

FUSED_TILES = 2
CHUNKS = (256, 256, 256, 128, 128)

KIB = 1024
W1_AT, W2_AT, E_SCALES_AT = 0, 8 * KIB, 16 * KIB
E_WORDS_AT, BOUNDS_AT, WT_AT, W3_AT, UNIT_AT = 18 * KIB, 26 * KIB, 42 * KIB, 58 * KIB, 60 * KIB
X_WORDS_AT = 64 * KIB
FIRST_HELD = (W1_AT, E_WORDS_AT)
SECOND_HELD = (E_WORDS_AT, 62 * KIB)
ROW_BYTES = 4 * S


def tile_picked_ydapol_tok_p_kernel(
    tc, x_words, x_scales, w1, e_words, e_scales, w2, lo, hi, wt, unit, w3, offs, twin, mini, out
):
    nc = tc.nc
    with ExitStack() as ctx:
        keep = ctx.enter_context(tc.tile_pool(name="keep", bufs=1))
        work = ctx.enter_context(tc.tile_pool(name="work", bufs=2))
        loads = ctx.enter_context(tc.tile_pool(name="loads", bufs=1))
        psum = ctx.enter_context(tc.psum_pool(name="psum", bufs=1))

        def load_words(words, name, offset):
            table = loads.tile([P, T], I32, name=name, offset=offset)
            nc.sync.dma_start(table[:], words[0].rearrange("p c r -> p (c r)").bitcast(I32))
            return table

        def load_scales(scales, table, engine):
            engine.memset(table[:].bitcast(I32), 0)
            for q in range(QUADRANTS):
                nc.sync.dma_start(
                    table[32 * q : 32 * q + 4, :].bitcast(I32), scales[0, 4 * q : 4 * q + 4, :].bitcast(I32)
                )
            return table

        def load_list(src, name):
            entries = keep.tile([P, src.shape[1]], U16, name=name)
            nc.sync.dma_start(entries[:], src)
            return entries

        def load_weight(src, name, offset):
            rows = loads.tile([P, PACK, src.shape[1]], F32, name=name, offset=offset)
            nc.sync.dma_start(rows[:], src.rearrange("(p j) c -> p j c", j=PACK))
            return rows

        def load_hidden_tile(src, t, name, offset):
            rows = loads.tile([P, src.shape[1]], F32, name=name, offset=offset)
            nc.sync.dma_start(rows[:], src.rearrange("(p t) c -> t p c", t=PACK)[t])
            return rows

        def covering(span, name):
            return loads.tile([P, (span[1] - span[0]) // 4], F32, name=name, offset=span[0])

        def pick_scales(scale_table, entries, name, tag):
            scales = keep.tile([P, S], U8, name=name, tag=tag, align_bytes=64)
            nc.vector.tensor_copy(scales[:], scale_table[:].indirect(entries[:]))
            return scales

        def pick_codes(table, entries, name, tag, parts):
            codes = keep.tile([P, S], U32, name=name, tag=tag, align_bytes=64)
            width = S // parts
            for j0 in range(0, S, width):
                nc.vector.tensor_copy(
                    codes[:, j0 : j0 + width],
                    table[:].bitcast(U32).indirect(entries[:, j0 // STRIPE : (j0 + width) // STRIPE]),
                )
            return codes

        def quantize(grouped, codes, name, pool):
            scales = pool.tile([P, codes.shape[1]], U8, name=name + "_scales", align_bytes=64)
            nc.vector.quantize_mx(out=codes[:].bitcast(FP8X4), scales=scales[:], in_=grouped)
            return codes, scales

        def negated_copy(dst, src):
            nc.scalar.activation(dst, src, ACT.Copy, scale=-1.0)

        def plain_copy(dst, src):
            nc.scalar.activation(dst, src, ACT.Copy, scale=1.0)

        def quantize_weight_pair(raw, pair, name, interleave, tag, codes_pool, codes_offset):
            grouped = keep.tile([P, 2, P, PACK], BF16, name=name + "_grouped", tag=tag, align_bytes=64)
            interleave(
                grouped[:].rearrange("p t m j -> p m j t"),
                raw[:].rearrange("p j (m t) -> p m j t", t=PACK)[:, :, :, 2 * pair : 2 * pair + 2],
            )
            codes = codes_pool.tile([P, 2 * P], U32, name=name + "_codes", align_bytes=64, offset=codes_offset)
            return quantize(grouped[:].rearrange("p t m j -> p (t m j)"), codes, name, keep)

        def product(acc, weight_pairs, t, picked, start, stop, tokens=slice(0, S)):
            codes, scales = weight_pairs[t // 2]
            channels = slice((t % 2) * P, (t % 2 + 1) * P)
            nc.tensor.matmul_mx(
                out=acc[:],
                lhsT=codes[:, channels].bitcast(FP8X4),
                lhsT_scale=scales[:, channels],
                rhs=picked[0][:, tokens].bitcast(FP8X4),
                rhs_scale=picked[1][:, tokens],
                start=start,
                stop=stop,
            )

        offs_sb = load_list(offs, "offs_sb")
        twin_sb = load_list(twin, "twin_sb")
        mini_sb = load_list(mini, "mini_sb")
        x_table = load_words(x_words, "x_table", X_WORDS_AT)
        x_scale_table = load_scales(x_scales, keep.tile([P, T], U8, name="x_scale_table"), nc.vector)
        x_picked_scales = pick_scales(x_scale_table, offs_sb, "x_picked_scales", "x_picked_scales")
        ones = covering(FIRST_HELD, "ones")
        diagonal = covering(SECOND_HELD, "diagonal")
        identity = keep.tile([P, P], F32, name="identity")
        nc.gpsimd.memset(ones[:, :P], 1.0)
        nc.gpsimd.affine_select(
            out=diagonal[:, :P],
            in_=ones[:, :P],
            pattern=[[-1, P]],
            compare_op=ALU.is_equal,
            fill=0.0,
            base=0,
            channel_multiplier=1,
        )
        w1_raw = load_weight(w1, "w1_raw", W1_AT)
        w2_raw = load_weight(w2, "w2_raw", W2_AT)
        e_scale_table = load_scales(
            e_scales, loads.tile([P, T], U8, name="e_scale_table", offset=E_SCALES_AT), nc.gpsimd
        )
        nc.scalar.activation(identity[:], diagonal[:, :P], ACT.Copy)
        e_table = load_words(e_words, "e_table", E_WORDS_AT)
        lo_sb, hi_sb = [], []
        for t in range(PACK):
            lo_sb.append(load_hidden_tile(lo, t, "lo%d" % t, BOUNDS_AT + 2 * t * ROW_BYTES))
            hi_sb.append(load_hidden_tile(hi, t, "hi%d" % t, BOUNDS_AT + (2 * t + 1) * ROW_BYTES))
        unit_sb = loads.tile([P, PACK], F32, name="unit_sb", offset=UNIT_AT)
        nc.sync.dma_start(unit_sb[:], unit.rearrange("(p t) o -> p (t o)", t=PACK))
        wt_sb = [load_hidden_tile(wt, t, "wt%d" % t, WT_AT + t * 4 * U) for t in range(PACK)]
        w3_raw = load_weight(w3, "w3_raw", W3_AT)

        x_picked = (pick_codes(x_table, offs_sb, "x_picked_codes", "x_picked_codes", 1), x_picked_scales)
        w1_pairs = [
            quantize_weight_pair(w1_raw, 0, "w1_0", nc.vector.tensor_copy, "grouped0", keep, None),
            quantize_weight_pair(w1_raw, 1, "w1_1", plain_copy, "grouped1", keep, None),
        ]

        y_banks, y_sb, totals, adv = [], {}, [], []

        def group_sum(t):
            y = psum.tile([P, S], F32, name="y%d" % t)
            product(y, w1_pairs, t, x_picked, True, True)
            y_banks.append(y)
            if t < FUSED_TILES:
                total = keep.tile([P, S // D], F32, name="total%d" % t, align_bytes=64)
                nc.vector.tensor_reduce(
                    total[:], y[:].rearrange("p (v d) -> p v d", d=D), mybir.AxisListType.X, ALU.add
                )
            else:
                y_sb[t] = loads.tile([P, S], F32, name="y_sb%d" % t, offset=W2_AT + (t - FUSED_TILES) * ROW_BYTES)
                nc.scalar.copy(y_sb[t][:], y[:])
                total = keep.tile([P, S // D], F32, name="total%d" % t, align_bytes=64)
                members = y_sb[t][:].rearrange("p (v d) -> p v d", d=D)
                half_sums = work.tile([P, S // D, 2], F32, name="pairs")
                nc.gpsimd.tensor_tensor(half_sums[:], members[:, :, 0:2], members[:, :, 2:4], ALU.add)
                nc.gpsimd.tensor_tensor(total[:], half_sums[:, :, 0], half_sums[:, :, 1], ALU.add)
            totals.append(total)

        def advantage(t, pool, offset):
            values = pool.tile([P, S], F32, name="adv%d" % t, offset=offset)
            nc.vector.scalar_tensor_tensor(
                values[:].rearrange("p (v d) -> p v d", d=D),
                totals[t][:].unsqueeze(2).to_broadcast([P, S // D, D]),
                -1.0 / D,
                y_banks[t][:].rearrange("p (v d) -> p v d", d=D),
                ALU.mult,
                ALU.add,
            )
            adv.append(values)

        group_sum(0)
        group_sum(1)
        advantage(0, keep, None)
        e_picked_scales = pick_scales(e_scale_table, twin_sb, "e_picked_scales", "total0")
        minus_w2_pairs = [quantize_weight_pair(w2_raw, 0, "w2_0", negated_copy, "grouped1", keep, None)]
        e_picked = (pick_codes(e_table, twin_sb, "e_picked_codes", "grouped1", 2), e_picked_scales)
        advantage(1, loads, E_WORDS_AT)
        minus_w2_pairs.append(
            quantize_weight_pair(w2_raw, 1, "w2_1", negated_copy, "grouped2", loads, E_WORDS_AT + 3 * ROW_BYTES)
        )
        group_sum(2)
        group_sum(3)
        advantage(2, loads, E_WORDS_AT + ROW_BYTES)
        advantage(3, loads, E_WORDS_AT + 2 * ROW_BYTES)

        def transposed_sum(acc, terms):
            for b in range(S // P):
                block = slice(b * P, (b + 1) * P)
                for index, term in enumerate(terms):
                    nc.tensor.matmul(
                        acc[:, block],
                        term[:, block],
                        identity[:],
                        start=index == 0,
                        stop=index == len(terms) - 1,
                        is_transpose=True,
                    )

        def exp_tanh(parts, t):
            bounded = keep.tile([P, S], F32, name="bounded%d" % t, align_bytes=64)
            values = keep.tile([P, S], F32, name="ratio%d" % t)
            for diff, tokens in parts:
                nc.scalar.activation(bounded[:, tokens], diff[:], ACT.Tanh)
                nc.scalar.activation(values[:, tokens], bounded[:, tokens], ACT.Exp, scale=0.8)
            return values

        ratio = []
        for t, banks in enumerate((("diff0", "y0"), ("diff1",))):
            parts = []
            width = S // len(banks)
            for half, bank in enumerate(banks):
                tokens = slice(half * width, (half + 1) * width)
                diff = psum.tile([P, width], F32, name="diff", tag=bank)
                product(diff, w1_pairs, t, x_picked, True, False, tokens)
                product(diff, minus_w2_pairs, t, e_picked, False, True, tokens)
                parts.append((diff, tokens))
            ratio.append(exp_tanh(parts, t))
        minus_ye = {}
        for t in range(FUSED_TILES, PACK):
            minus_ye_bank = psum.tile([P, S], F32, name="minus_ye", tag="out%d" % (t % 2))
            product(minus_ye_bank, minus_w2_pairs, t, e_picked, True, True)
            minus_ye[t] = keep.tile([P, S], F32, name="minus_ye_sb%d" % t)
            nc.scalar.copy(minus_ye[t][:], minus_ye_bank[:])
        for t in range(FUSED_TILES, PACK):
            diff_turned = psum.tile([P, S], F32, name="diff_turned", tag="y%d" % (t % 2))
            transposed_sum(diff_turned, [y_sb[t], minus_ye[t]])
            ratio_bank = psum.tile([P, S], F32, name="ratio_bank", tag="diff%d" % (t % 2))
            transposed_sum(ratio_bank, [exp_tanh([(diff_turned, slice(0, S))], t)])
            ratio.append(ratio_bank)

        floored, plain, clip, clipped, sur = {}, {}, {}, {}, {}

        def step(results, name, t, first, second, op):
            if 0 <= t < PACK:
                results[t] = keep.tile([P, S], F32, name=name % t)
                nc.vector.tensor_tensor(results[t][:], first[t][:], second[t][:], op)

        for t in range(PACK + 1):
            step(floored, "floored%d", t, ratio, lo_sb, ALU.max)
            step(clipped, "clipped%d", t - 1, clip, adv, ALU.mult)
            step(plain, "plain%d", t, ratio, adv, ALU.mult)
            step(sur, "sur%d", t - 1, plain, clipped, ALU.min)
            step(clip, "clip%d", t, floored, hi_sb, ALU.min)

        weight = keep.tile([P, PACK, U], F32, name="weight", tag="bounded3", align_bytes=64)
        for t in range(PACK):
            nc.scalar.activation(weight[:, t, :], wt_sb[t][:], ACT.Copy, scale=unit_sb[:, t : t + 1])

        w3_grouped = keep.tile([P, N, PACK], BF16, name="w3_grouped", tag="bounded2", align_bytes=64)
        nc.scalar.copy(
            w3_grouped[:].rearrange("p (c i) j -> p c j i", i=LINE),
            w3_raw[:].rearrange("p j (c i) -> p c j i", i=LINE),
        )
        w3_codes = keep.tile([P, N], U32, name="w3_codes", align_bytes=64)
        w3_codes, w3_scales = quantize(w3_grouped[:].rearrange("p m j -> p (m j)"), w3_codes, "w3", keep)

        r0 = 0
        for c, width in enumerate(CHUNKS):
            copy = nc.vector.tensor_copy if c == len(CHUNKS) - 1 else nc.scalar.copy
            hid = work.tile([P, PACK, width], F32, name="hid")
            for t in range(PACK):
                nc.vector.tensor_tensor(
                    hid[:, t, :],
                    sur[t][:].indirect(mini_sb[:, r0 // STRIPE : (r0 + width) // STRIPE]),
                    weight[:, t, r0 : r0 + width],
                    ALU.mult,
                )
            hid_grouped = work.tile([P, width, PACK], BF16, name="hid_grouped", align_bytes=64)
            copy(
                hid_grouped[:].rearrange("p (c i) t -> p c t i", i=LINE),
                hid[:].rearrange("p t (c i) -> p c t i", i=LINE),
            )
            hid_codes = work.tile([P, width], U32, name="hid_codes", align_bytes=64)
            hid_codes, hid_scales = quantize(hid_grouped[:].rearrange("p r t -> p (r t)"), hid_codes, "hid", work)
            out_bank = psum.tile([P, width], F32, name="out%d" % (c % 2))
            nc.tensor.matmul_mx(
                out=out_bank[:],
                lhsT=w3_codes[:].bitcast(FP8X4),
                lhsT_scale=w3_scales[:],
                rhs=hid_codes[:].bitcast(FP8X4),
                rhs_scale=hid_scales[:],
                start=True,
                stop=True,
            )
            result = work.tile([P, width], F32, name="result")
            copy(result[:], out_bank[:])
            nc.sync.dma_start(out[:, r0 : r0 + width], result[:])
            r0 += width
